import numpy as np
CORES = [12,28,60,100,156,228]
N = 6
CB = 64
def setup_inputs(rng):
    return {"x": rng.standard_normal((N, 128, N * CB), dtype=np.float32)}
def setup_inputs_big(rng):
    d = setup_inputs(rng)
    for k in ("x",): d[k] = (d[k].astype(np.float32) * 1024.0).astype(d[k].dtype)
    return d
def setup_inputs_small(rng):
    d = setup_inputs(rng)
    for k in ("x",): d[k] = (d[k].astype(np.float32) * (1 / 1024.0)).astype(d[k].dtype)
    return d
def setup_inputs_apart(rng):
    d = setup_inputs(rng)
    f = (10.0 ** rng.permutation(np.linspace(-1.5, 1.5, N))).astype(np.float32).reshape(N, 1, 1)
    for k in ("x",): d[k] = (d[k].astype(np.float32) * f).astype(d[k].dtype)
    return d
def reference(x):
    X = x.astype(np.float64)
    G = sum(X[j].T @ X[j] for j in range(N))
    y = np.full((N, CB, N * CB), np.nan)
    for r in range(N):
        y[r][:, :CB * r] = G[CB * r:CB * r + CB, :CB * r]
    return {"y": y.astype(np.float32 if x.dtype != np.float64 else np.float64)}

@@ -1,0 +1,165 @@
+from concourse.bass import DstId, RemoteDMATransfer
+from concourse.mybir import AluOpType
+
+WORLD = 256
+N = 6
+CB = 64
+HALF = CB // 2
+SLOT = HALF * (N - 1)
+NSLOT = 4
+
+
+def _w(d):
+    return HALF * d
+
+
+def _off(d):
+    return HALF * d * (d - 1) // 2
+
+
+SCRATCH = {
+    "xs": ("sbuf", [128, N * CB], "float32"),
+    "stage": ("sbuf", [128, _off(N)], "float32"),
+    "land": ("sbuf", [128, NSLOT * SLOT], "float32"),
+    "acc": ("sbuf", [128, SLOT], "float32"),
+}
+for _d in range(1, N):
+    SCRATCH["ps%d" % _d] = ("psum", [128, 512], "float32")
+
+SEMAPHORES = (["ld", "sent", "harr", "ac", "st"] + ["mm%d" % d for d in range(1, N)] + ["cp%d" % d for d in range(1, N)]
+              + ["arr%d" % k for k in range(NSLOT)])
+
+
+def _pop(m):
+    return sum((m >> b) & 1 for b in range(16))
+
+
+def _same_chip(topo, a, b):
+    return topo.host(a) == topo.host(b) and topo.chip(a) == topo.chip(b)
+
+
+def _mask(topo, src, dst):
+    full = topo.mask(src, dst)
+    if _same_chip(topo, src, dst):
+        away = 0
+        for c in range(WORLD):
+            if topo.same_plane(src, c):
+                away = topo.mask(src, c)
+                break
+        if full & ~away:
+            return full & ~away
+    return full
+
+
+def _helper(topo, home, dst, used):
+    cand = [c for c in range(WORLD) if _same_chip(topo, c, home) and c not in used and topo.may_write(c, dst)]
+    cand.sort(key=lambda c: (topo.die(c) != topo.die(home), c))
+    return cand[0]
+
+
+def _plan(cores, topo):
+    n = len(cores)
+    used = set(cores)
+    hosted = [0] * n
+    sends = dict((j, []) for j in range(n))
+    helpers = {}
+    arrivals = dict((d, []) for d in range(n))
+    for d in range(n - 1, 0, -1):
+        near = [j for j in range(n) if j != d and topo.may_write(cores[j], cores[d])]
+        far = [j for j in range(n) if j != d and not topo.may_write(cores[j], cores[d])]
+        for j in near:
+            k = len(arrivals[d])
+            arrivals[d].append(cores[j])
+            sends[j].append({"d": d, "to": cores[d], "slot": k, "sem": "arr%d" % k, "hops": 1})
+        for p in range(0, len(far), 2):
+            pair = far[p:p + 2]
+            home = min(pair, key=lambda j: (hosted[j], j))
+            hosted[home] += _w(d)
+            h = _helper(topo, cores[home], cores[d], used)
+            used.add(h)
+            k = len(arrivals[d])
+            arrivals[d].append(h)
+            helpers[h] = {"d": d, "srcs": [cores[j] for j in pair], "slot": k}
+            for i, j in enumerate(pair):
+                sends[j].append({"d": d, "to": h, "slot": i, "sem": "harr", "hops": 2})
+    for j in range(n):
+        sends[j].sort(key=lambda s: (-s["hops"], -s["d"]))
+    return sends, helpers, arrivals
+
+
+def _slot(T, k, w):
+    return T.land[:, SLOT * k:SLOT * k + w]
+
+
+def _helper_program(g, core, T, topo, job):
+    S = T.sem
+    d = job["d"]
+    w = _w(d)
+    dst = T.cores[d]
+    g.wait_ge(S.harr, sum(_pop(_mask(topo, s, core)) for s in job["srcs"]))
+    rid, pid = topo.addr(dst, core)
+    m = _mask(topo, core, dst)
+    k = job["slot"]
+    n = len(job["srcs"])
+    if n == 1:
+        g.remote_dma(out_ap=_slot(T, k, w), in_ap=_slot(T, 0, w), remote_sem=S["arr%d" % k], local_sem=S.sent,
+                     pid=pid, routing_id=rid, dma_engine_mask=m)
+    else:
+        g.remote_dma_fused([RemoteDMATransfer(dst_ids=[DstId(rid=rid, pnc=pid)], dma_engine_mask=m,
+                                              remote_sem=S["arr%d" % k], srcs=[_slot(T, i, w) for i in range(n)],
+                                              dsts=[_slot(T, k, w)], alu_op=1)], local_sem=S.sent)
+    g.wait_ge(S.sent, _pop(m))
+
+
+def rank_program(g, core, T, topo):
+    S = T.sem
+    sends, helpers, arrivals = _plan(T.cores, topo)
+    rank = T.rank_of(core)
+    if rank is None:
+        if core in helpers:
+            _helper_program(g, core, T, topo, helpers[core])
+        return
+
+    g.sync.dma_start(T.xs[:], T.x[:]).then_inc(S.ld, 16)
+
+    order = [s["d"] for s in sends[rank]] + ([rank] if rank >= 1 else [])
+    g.tensor.wait_ge(S.ld, 16)
+    for d in order:
+        w = _w(d)
+        ps = T["ps%d" % d]
+        blk = T.xs[:, CB * d:CB * d + CB]
+        g.tensor.matmul(ps[0:CB, 0:w], blk, T.xs[:, 0:w], True, True).then_inc(S["mm%d" % d], 1)
+        g.tensor.matmul(ps[CB:2 * CB, 0:w], blk, T.xs[:, w:2 * w], True, True).then_inc(S["mm%d" % d], 1)
+
+    total = 0
+    for s in sends[rank]:
+        d = s["d"]
+        w = _w(d)
+        piece = T.stage[:, _off(d):_off(d) + w]
+        g.vector.wait_ge(S["mm%d" % d], 2)
+        g.vector.tensor_copy(piece, T["ps%d" % d][:, 0:w]).then_inc(S["cp%d" % d], 1)
+        rid, pid = topo.addr(s["to"], core)
+        m = _mask(topo, core, s["to"])
+        g.wait_ge(S["cp%d" % d], 1)
+        g.remote_dma(out_ap=_slot(T, s["slot"], w), in_ap=piece, remote_sem=S[s["sem"]], local_sem=S.sent,
+                     pid=pid, routing_id=rid, dma_engine_mask=m)
+        total += _pop(m)
+    g.wait_ge(S.sent, total)
+
+    if rank < 1:
+        return
+    w = _w(rank)
+    acc = T.acc[:, 0:w]
+    g.vector.wait_ge(S["mm%d" % rank], 2)
+    for k, src in enumerate(arrivals[rank]):
+        g.vector.wait_ge(S["arr%d" % k], _pop(_mask(topo, src, core)))
+        if k:
+            g.vector.wait_ge(S.ac, k)
+        g.vector.tensor_tensor(acc, T["ps%d" % rank][:, 0:w] if k == 0 else acc, _slot(T, k, w),
+                               AluOpType.add).then_inc(S.ac, 1)
+    n = len(arrivals[rank])
+    g.sync.wait_ge(S.ac, n)
+    g.sync.dma_start(T.y[:, 0:w], T.acc[0:CB, 0:w]).then_inc(S.st, 16)
+    g.scalar.wait_ge(S.ac, n)
+    g.scalar.dma_start(T.y[:, w:2 * w], T.acc[CB:2 * CB, 0:w]).then_inc(S.st, 16)
+    g.wait_ge(S.st, 32)

@@ -7,6 +7,7 @@ CB = 64
 HALF = CB // 2
 SLOT = HALF * (N - 1)
 NSLOT = 4
+WIDE = 3 * HALF
 
 
 def _w(d):
@@ -22,12 +23,13 @@ SCRATCH = {
     "stage": ("sbuf", [128, _off(N)], "float32"),
     "land": ("sbuf", [128, NSLOT * SLOT], "float32"),
     "acc": ("sbuf", [128, SLOT], "float32"),
+    "psx": ("psum", [128, 512], "float32"),
 }
 for _d in range(1, N):
     SCRATCH["ps%d" % _d] = ("psum", [128, 512], "float32")
 
-SEMAPHORES = (["ld", "sent", "harr", "ac", "st"] + ["mm%d" % d for d in range(1, N)] + ["cp%d" % d for d in range(1, N)]
-              + ["arr%d" % k for k in range(NSLOT)])
+SEMAPHORES = (["ld", "sent", "harr", "ac", "st", "mmx", "cpx"] + ["mm%d" % d for d in range(1, N)]
+              + ["cp%d" % d for d in range(1, N)] + ["arr%d" % k for k in range(NSLOT)])
 
 
 def _pop(m):
@@ -65,49 +67,52 @@ def _plan(cores, topo):
     helpers = {}
     arrivals = dict((d, []) for d in range(n))
     for d in range(n - 1, 0, -1):
+        w = _w(d)
         near = [j for j in range(n) if j != d and topo.may_write(cores[j], cores[d])]
         far = [j for j in range(n) if j != d and not topo.may_write(cores[j], cores[d])]
         for j in near:
             k = len(arrivals[d])
-            arrivals[d].append(cores[j])
-            sends[j].append({"d": d, "to": cores[d], "slot": k, "sem": "arr%d" % k, "hops": 1})
+            arrivals[d].append([cores[j]])
+            sends[j].append({"d": d, "hops": 1, "parts": [(0, w, cores[d], SLOT * k, "arr%d" % k)]})
         for p in range(0, len(far), 2):
             pair = far[p:p + 2]
-            home = min(pair, key=lambda j: (hosted[j], j))
-            hosted[home] += _w(d)
-            h = _helper(topo, cores[home], cores[d], used)
-            used.add(h)
             k = len(arrivals[d])
-            arrivals[d].append(h)
-            helpers[h] = {"d": d, "srcs": [cores[j] for j in pair], "slot": k}
-            for i, j in enumerate(pair):
-                sends[j].append({"d": d, "to": h, "slot": i, "sem": "harr", "hops": 2})
+            if w >= WIDE and len(pair) == 2:
+                homes = pair
+            else:
+                homes = [min(pair, key=lambda j: (hosted[j], j))]
+                hosted[homes[0]] += w
+            step = w // len(homes)
+            hs = []
+            parts = dict((j, []) for j in pair)
+            for q, home in enumerate(homes):
+                h = _helper(topo, cores[home], cores[d], used)
+                used.add(h)
+                hs.append(h)
+                helpers[h] = {"d": d, "c0": q * step, "c1": (q + 1) * step, "srcs": [cores[j] for j in pair], "slot": k}
+                for i, j in enumerate(pair):
+                    parts[j].append((q * step, (q + 1) * step, h, SLOT * i, "harr"))
+            arrivals[d].append(hs)
+            for j in pair:
+                sends[j].append({"d": d, "hops": 2, "parts": parts[j]})
     for j in range(n):
         sends[j].sort(key=lambda s: (-s["hops"], -s["d"]))
     return sends, helpers, arrivals
 
 
-def _slot(T, k, w):
-    return T.land[:, SLOT * k:SLOT * k + w]
-
-
 def _helper_program(g, core, T, topo, job):
     S = T.sem
-    d = job["d"]
-    w = _w(d)
-    dst = T.cores[d]
+    dst = T.cores[job["d"]]
+    c0, c1 = job["c0"], job["c1"]
     g.wait_ge(S.harr, sum(_pop(_mask(topo, s, core)) for s in job["srcs"]))
     rid, pid = topo.addr(dst, core)
     m = _mask(topo, core, dst)
     k = job["slot"]
     n = len(job["srcs"])
-    if n == 1:
-        g.remote_dma(out_ap=_slot(T, k, w), in_ap=_slot(T, 0, w), remote_sem=S["arr%d" % k], local_sem=S.sent,
-                     pid=pid, routing_id=rid, dma_engine_mask=m)
-    else:
-        g.remote_dma_fused([RemoteDMATransfer(dst_ids=[DstId(rid=rid, pnc=pid)], dma_engine_mask=m,
-                                              remote_sem=S["arr%d" % k], srcs=[_slot(T, i, w) for i in range(n)],
-                                              dsts=[_slot(T, k, w)], alu_op=1)], local_sem=S.sent)
+    g.remote_dma_fused([RemoteDMATransfer(dst_ids=[DstId(rid=rid, pnc=pid)], dma_engine_mask=m,
+                                          remote_sem=S["arr%d" % k],
+                                          srcs=[T.land[:, SLOT * i:SLOT * i + c1 - c0] for i in range(n)],
+                                          dsts=[T.land[:, SLOT * k + c0:SLOT * k + c1]], alu_op=1)], local_sem=S.sent)
     g.wait_ge(S.sent, _pop(m))
 
 
@@ -122,42 +127,56 @@ def rank_program(g, core, T, topo):
 
     g.sync.dma_start(T.xs[:], T.x[:]).then_inc(S.ld, 16)
 
-    order = [s["d"] for s in sends[rank]] + ([rank] if rank >= 1 else [])
+    units, calls = [], []
+    for i, s in enumerate(sends[rank]):
+        d = s["d"]
+        if i == 0 and len(s["parts"]) == 2:
+            (a0, a1), (b0, b1) = s["parts"][0][0:2], s["parts"][1][0:2]
+            units.append((d, a0, a1, "ps%d" % d, "mm%d" % d, "cp%d" % d))
+            units.append((d, b0, b1, "psx", "mmx", "cpx"))
+            calls.append(("cp%d" % d, d, s["parts"][0:1]))
+            calls.append(("cpx", d, s["parts"][1:2]))
+        else:
+            units.append((d, 0, _w(d), "ps%d" % d, "mm%d" % d, "cp%d" % d))
+            calls.append(("cp%d" % d, d, s["parts"]))
+
     g.tensor.wait_ge(S.ld, 16)
-    for d in order:
+    for d, c0, c1, bank, mm, cp in units + ([(rank, 0, _w(rank), "ps%d" % rank, "mm%d" % rank, None)] if rank >= 1 else []):
         w = _w(d)
-        ps = T["ps%d" % d]
         blk = T.xs[:, CB * d:CB * d + CB]
-        g.tensor.matmul(ps[0:CB, 0:w], blk, T.xs[:, 0:w], True, True).then_inc(S["mm%d" % d], 1)
-        g.tensor.matmul(ps[CB:2 * CB, 0:w], blk, T.xs[:, w:2 * w], True, True).then_inc(S["mm%d" % d], 1)
+        g.tensor.matmul(T[bank][0:CB, 0:c1 - c0], blk, T.xs[:, c0:c1], True, True).then_inc(S[mm], 1)
+        g.tensor.matmul(T[bank][CB:2 * CB, 0:c1 - c0], blk, T.xs[:, w + c0:w + c1], True, True).then_inc(S[mm], 1)
+
+    for d, c0, c1, bank, mm, cp in units:
+        g.vector.wait_ge(S[mm], 2)
+        g.vector.tensor_copy(T.stage[:, _off(d) + c0:_off(d) + c1], T[bank][:, 0:c1 - c0]).then_inc(S[cp], 1)
 
     total = 0
-    for s in sends[rank]:
-        d = s["d"]
-        w = _w(d)
-        piece = T.stage[:, _off(d):_off(d) + w]
-        g.vector.wait_ge(S["mm%d" % d], 2)
-        g.vector.tensor_copy(piece, T["ps%d" % d][:, 0:w]).then_inc(S["cp%d" % d], 1)
-        rid, pid = topo.addr(s["to"], core)
-        m = _mask(topo, core, s["to"])
-        g.wait_ge(S["cp%d" % d], 1)
-        g.remote_dma(out_ap=_slot(T, s["slot"], w), in_ap=piece, remote_sem=S[s["sem"]], local_sem=S.sent,
-                     pid=pid, routing_id=rid, dma_engine_mask=m)
-        total += _pop(m)
+    for cp, d, parts in calls:
+        g.wait_ge(S[cp], 1)
+        trs = []
+        for c0, c1, to, at, sem in parts:
+            rid, pid = topo.addr(to, core)
+            m = _mask(topo, core, to)
+            total += _pop(m)
+            trs.append(RemoteDMATransfer(dst_ids=[DstId(rid=rid, pnc=pid)], dma_engine_mask=m, remote_sem=S[sem],
+                                         srcs=[T.stage[:, _off(d) + c0:_off(d) + c1]],
+                                         dsts=[T.land[:, at:at + c1 - c0]], alu_op=0))
+        g.remote_dma_fused(trs, local_sem=S.sent)
     g.wait_ge(S.sent, total)
 
     if rank < 1:
         return
     w = _w(rank)
-    acc = T.acc[:, 0:w]
+    own = T["ps%d" % rank][:, 0:w]
+    n = len(arrivals[rank])
     g.vector.wait_ge(S["mm%d" % rank], 2)
-    for k, src in enumerate(arrivals[rank]):
-        g.vector.wait_ge(S["arr%d" % k], _pop(_mask(topo, src, core)))
+    for k, srcs in enumerate(arrivals[rank]):
+        g.vector.wait_ge(S["arr%d" % k], sum(_pop(_mask(topo, src, core)) for src in srcs))
         if k:
             g.vector.wait_ge(S.ac, k)
-        g.vector.tensor_tensor(acc, T["ps%d" % rank][:, 0:w] if k == 0 else acc, _slot(T, k, w),
+        g.vector.tensor_tensor(T.acc[:, 0:w] if k == n - 1 else own, own, T.land[:, SLOT * k:SLOT * k + w],
                                AluOpType.add).then_inc(S.ac, 1)
-    n = len(arrivals[rank])
     g.sync.wait_ge(S.ac, n)
     g.sync.dma_start(T.y[:, 0:w], T.acc[0:CB, 0:w]).then_inc(S.st, 16)
     g.scalar.wait_ge(S.ac, n)

from concourse.bass import DstId, RemoteDMATransfer
from concourse.mybir import AluOpType

WORLD = 256
N = 6
CB = 64
HALF = CB // 2
SLOT = HALF * (N - 1)
NSLOT = 4
WIDE = 3 * HALF


def _w(d):
    return HALF * d


def _off(d):
    return HALF * d * (d - 1) // 2


SCRATCH = {
    "xs": ("sbuf", [128, N * CB], "float32"),
    "stage": ("sbuf", [128, _off(N)], "float32"),
    "land": ("sbuf", [128, NSLOT * SLOT], "float32"),
    "acc": ("sbuf", [128, SLOT], "float32"),
    "psx": ("psum", [128, 512], "float32"),
}
for _d in range(1, N):
    SCRATCH["ps%d" % _d] = ("psum", [128, 512], "float32")

SEMAPHORES = (["ld", "sent", "harr", "ac", "st", "mmx", "cpx"] + ["mm%d" % d for d in range(1, N)]
              + ["cp%d" % d for d in range(1, N)] + ["arr%d" % k for k in range(NSLOT)])


def _pop(m):
    return sum((m >> b) & 1 for b in range(16))


def _same_chip(topo, a, b):
    return topo.host(a) == topo.host(b) and topo.chip(a) == topo.chip(b)


def _mask(topo, src, dst):
    full = topo.mask(src, dst)
    if _same_chip(topo, src, dst):
        away = 0
        for c in range(WORLD):
            if topo.same_plane(src, c):
                away = topo.mask(src, c)
                break
        if full & ~away:
            return full & ~away
    return full


def _helper(topo, home, dst, used):
    cand = [c for c in range(WORLD) if _same_chip(topo, c, home) and c not in used and topo.may_write(c, dst)]
    cand.sort(key=lambda c: (topo.die(c) != topo.die(home), c))
    return cand[0]


def _plan(cores, topo):
    n = len(cores)
    used = set(cores)
    hosted = [0] * n
    sends = dict((j, []) for j in range(n))
    helpers = {}
    arrivals = dict((d, []) for d in range(n))
    for d in range(n - 1, 0, -1):
        w = _w(d)
        near = [j for j in range(n) if j != d and topo.may_write(cores[j], cores[d])]
        far = [j for j in range(n) if j != d and not topo.may_write(cores[j], cores[d])]
        for j in near:
            k = len(arrivals[d])
            arrivals[d].append([cores[j]])
            sends[j].append({"d": d, "hops": 1, "parts": [(0, w, cores[d], SLOT * k, "arr%d" % k)]})
        for p in range(0, len(far), 2):
            pair = far[p:p + 2]
            k = len(arrivals[d])
            if w >= WIDE and len(pair) == 2:
                homes = pair
            else:
                homes = [min(pair, key=lambda j: (hosted[j], j))]
                hosted[homes[0]] += w
            step = w // len(homes)
            hs = []
            parts = dict((j, []) for j in pair)
            for q, home in enumerate(homes):
                h = _helper(topo, cores[home], cores[d], used)
                used.add(h)
                hs.append(h)
                helpers[h] = {"d": d, "c0": q * step, "c1": (q + 1) * step, "srcs": [cores[j] for j in pair], "slot": k}
                for i, j in enumerate(pair):
                    parts[j].append((q * step, (q + 1) * step, h, SLOT * i, "harr"))
            arrivals[d].append(hs)
            for j in pair:
                sends[j].append({"d": d, "hops": 2, "parts": parts[j]})
    for j in range(n):
        sends[j].sort(key=lambda s: (-s["hops"], -s["d"]))
    return sends, helpers, arrivals


def _helper_program(g, core, T, topo, job):
    S = T.sem
    dst = T.cores[job["d"]]
    c0, c1 = job["c0"], job["c1"]
    g.wait_ge(S.harr, sum(_pop(_mask(topo, s, core)) for s in job["srcs"]))
    rid, pid = topo.addr(dst, core)
    m = _mask(topo, core, dst)
    k = job["slot"]
    n = len(job["srcs"])
    g.remote_dma_fused([RemoteDMATransfer(dst_ids=[DstId(rid=rid, pnc=pid)], dma_engine_mask=m,
                                          remote_sem=S["arr%d" % k],
                                          srcs=[T.land[:, SLOT * i:SLOT * i + c1 - c0] for i in range(n)],
                                          dsts=[T.land[:, SLOT * k + c0:SLOT * k + c1]], alu_op=1)], local_sem=S.sent)
    g.wait_ge(S.sent, _pop(m))


def rank_program(g, core, T, topo):
    S = T.sem
    sends, helpers, arrivals = _plan(T.cores, topo)
    rank = T.rank_of(core)
    if rank is None:
        if core in helpers:
            _helper_program(g, core, T, topo, helpers[core])
        return

    g.sync.dma_start(T.xs[:], T.x[:]).then_inc(S.ld, 16)

    units, calls = [], []
    for i, s in enumerate(sends[rank]):
        d = s["d"]
        if i == 0 and len(s["parts"]) == 2:
            (a0, a1), (b0, b1) = s["parts"][0][0:2], s["parts"][1][0:2]
            units.append((d, a0, a1, "ps%d" % d, "mm%d" % d, "cp%d" % d))
            units.append((d, b0, b1, "psx", "mmx", "cpx"))
            calls.append(("cp%d" % d, d, s["parts"][0:1]))
            calls.append(("cpx", d, s["parts"][1:2]))
        else:
            units.append((d, 0, _w(d), "ps%d" % d, "mm%d" % d, "cp%d" % d))
            calls.append(("cp%d" % d, d, s["parts"]))

    g.tensor.wait_ge(S.ld, 16)
    for d, c0, c1, bank, mm, cp in units + ([(rank, 0, _w(rank), "ps%d" % rank, "mm%d" % rank, None)] if rank >= 1 else []):
        w = _w(d)
        blk = T.xs[:, CB * d:CB * d + CB]
        g.tensor.matmul(T[bank][0:CB, 0:c1 - c0], blk, T.xs[:, c0:c1], True, True).then_inc(S[mm], 1)
        g.tensor.matmul(T[bank][CB:2 * CB, 0:c1 - c0], blk, T.xs[:, w + c0:w + c1], True, True).then_inc(S[mm], 1)

    for d, c0, c1, bank, mm, cp in units:
        g.vector.wait_ge(S[mm], 2)
        g.vector.tensor_copy(T.stage[:, _off(d) + c0:_off(d) + c1], T[bank][:, 0:c1 - c0]).then_inc(S[cp], 1)

    total = 0
    for cp, d, parts in calls:
        g.wait_ge(S[cp], 1)
        trs = []
        for c0, c1, to, at, sem in parts:
            rid, pid = topo.addr(to, core)
            m = _mask(topo, core, to)
            total += _pop(m)
            trs.append(RemoteDMATransfer(dst_ids=[DstId(rid=rid, pnc=pid)], dma_engine_mask=m, remote_sem=S[sem],
                                         srcs=[T.stage[:, _off(d) + c0:_off(d) + c1]],
                                         dsts=[T.land[:, at:at + c1 - c0]], alu_op=0))
        g.remote_dma_fused(trs, local_sem=S.sent)
    g.wait_ge(S.sent, total)

    if rank < 1:
        return
    w = _w(rank)
    own = T["ps%d" % rank][:, 0:w]
    n = len(arrivals[rank])
    g.vector.wait_ge(S["mm%d" % rank], 2)
    for k, srcs in enumerate(arrivals[rank]):
        g.vector.wait_ge(S["arr%d" % k], sum(_pop(_mask(topo, src, core)) for src in srcs))
        if k:
            g.vector.wait_ge(S.ac, k)
        g.vector.tensor_tensor(T.acc[:, 0:w] if k == n - 1 else own, own, T.land[:, SLOT * k:SLOT * k + w],
                               AluOpType.add).then_inc(S.ac, 1)
    g.sync.wait_ge(S.ac, n)
    g.sync.dma_start(T.y[:, 0:w], T.acc[0:CB, 0:w]).then_inc(S.st, 16)
    g.scalar.wait_ge(S.ac, n)
    g.scalar.dma_start(T.y[:, w:2 * w], T.acc[CB:2 * CB, 0:w]).then_inc(S.st, 16)
    g.wait_ge(S.st, 32)
